import numpy as np
import ml_dtypes


def mxq(x, axis, fmt="e4m3"):
    dtype, down = {"e4m3": (ml_dtypes.float8_e4m3fn, 7), "e5m2": (ml_dtypes.float8_e5m2, 14)}[fmt]
    v = np.moveaxis(np.asarray(x, np.float32).astype(ml_dtypes.bfloat16).astype(np.float64), axis, -1)
    blocks = v.reshape(v.shape[:-1] + (-1, 32))
    amax = np.abs(blocks).max(-1, keepdims=True)
    byte = np.maximum(np.where(amax > 0, np.frexp(amax)[1] - 1 + 127, 0) - down, 1)
    scale = np.exp2(byte - 127.0)
    codes = (blocks / scale).astype(np.float32).astype(dtype).astype(np.float64)
    return np.moveaxis((codes * scale).reshape(v.shape), -1, axis)


WIDE = False


def mx_kscale(k):
    if not WIDE:
        return np.ones(k)
    levels = np.array([10, -10, 5, -5, 0])
    if k % 512:
        return np.exp2(np.random.permutation(np.resize(levels, k // 32))).repeat(32)
    a = np.empty((k // 512, 16))
    for p in range(k // 512):
        a[p, :8] = np.random.permutation(np.resize(levels, 8))
        for g in range(8):
            far = levels[np.abs(levels - a[p, g]) >= 10]
            a[p, g + 8] = far[np.random.randint(len(far))]
    return np.exp2(a.ravel()).repeat(32)


def f64(x):
    return np.asarray(x).astype(np.float64)


def striped(idx):
    return np.tile(idx.reshape(-1, 16).T, (8, 1)).astype(np.uint16)


def unstriped(offs):
    return offs[:16].T.reshape(-1).astype(np.int64)


E2M1 = np.array([0.0, 0.5, 1.0, 1.5, 2.0, 3.0, 4.0, 6.0, -0.0, -0.5, -1.0, -1.5, -2.0, -3.0, -4.0, -6.0])


def pack_weight(w, fmt):
    k, n = w.shape
    w = f64(np.asarray(w, np.float32).astype(ml_dtypes.bfloat16)).reshape(k // 32, 32, n)
    amax = np.abs(w).max(1)
    if fmt == "e4m3":
        byte = np.frexp(amax)[1] - 1 + 127 - 7
    else:
        mant, ex = np.frexp(amax / 6.0)
        byte = np.where(mant > 0.5, ex, ex - 1) + 127
    byte = np.clip(np.where(amax > 0, byte, 1), 1, 254)
    scaled = (w * np.exp2(127.0 - byte)[:, None, :]).reshape(k, n).astype(np.float32)
    by_word = np.ascontiguousarray(scaled.reshape(k // 512, 128, 4, n).transpose(0, 1, 3, 2))
    if fmt == "e4m3":
        words = by_word.astype(ml_dtypes.float8_e4m3fn).view(np.uint8)
    else:
        c = by_word.astype(ml_dtypes.float4_e2m1fn).view(np.uint8) & 0xF
        words = (c[..., 0::2] | (c[..., 1::2] << 4)).reshape(k // 512, 128, 2 * n)
    return np.ascontiguousarray(words), np.ascontiguousarray(byte.astype(np.uint8).reshape(k // 512, 16, n))


def unpack_weight(words, scales, fmt):
    g, _, n = scales.shape
    words = np.ascontiguousarray(words).reshape(g, 128, n, -1)
    if fmt == "e4m3":
        vals = words.view(ml_dtypes.float8_e4m3fn).astype(np.float64)
    else:
        nib = np.empty((g, 128, n, 4), np.uint8)
        nib[..., 0::2] = words & 0xF
        nib[..., 1::2] = words >> 4
        vals = E2M1[nib]
    vals = vals * np.repeat(np.exp2(scales.astype(np.float64) - 127.0), 8, axis=1)[..., None]
    return vals.transpose(0, 1, 3, 2).reshape(g * 512, n)


def silu(v):
    return v / (1.0 + np.exp(-np.maximum(v, -700.0)))


K, T, E, C, N = 2560, 1280, 8, 128, 128
K8 = 1024


def by_expert(wq, xq):
    return np.concatenate([wq[e].T @ xq[:, e * C:(e + 1) * C] for e in range(E)], axis=1)


def setup_inputs():
    n = np.random.standard_normal
    s = mx_kscale(K)[:, None]
    w = n((E, K, N)) / np.sqrt(K) / s[None]
    w8 = [pack_weight(m[:K8], "e4m3") for m in w]
    w4 = [pack_weight(m[K8:], "e2m1") for m in w]
    return {
        "xT": (n((K, T)) * s).astype(np.float32),
        "w8_words": np.stack([m[0] for m in w8]),
        "w8_scales": np.stack([m[1] for m in w8]),
        "w4_words": np.stack([m[0] for m in w4]),
        "w4_scales": np.stack([m[1] for m in w4]),
        "b": (0.3 * n((N, E))).astype(np.float32),
        "gate": np.tile(np.random.uniform(0.2, 1.0, E * C), (N, 1)).astype(np.float32),
        "offs": striped(np.random.permutation(T)[:E * C]),
        "dst": striped(np.random.permutation(T)[:E * C]),
    }


def reference(xT, w8_words, w8_scales, w4_words, w4_scales, b, gate, offs, dst):
    idx = unstriped(offs)
    w = np.stack([np.concatenate([unpack_weight(w8_words[e], w8_scales[e], "e4m3"), unpack_weight(w4_words[e], w4_scales[e], "e2m1")]) for e in range(E)])
    xq = mxq(f64(xT)[:, idx], 0, "e4m3")
    y = by_expert(w, xq)
    y = silu(y + np.repeat(f64(b), C, axis=1))
    out = np.zeros((N, T))
    out[:, unstriped(dst)] = f64(gate) * y
    return out

@@ -1,0 +1,178 @@
+from contextlib import ExitStack
+
+import concourse.mybir as mybir
+
+K, T, E, C, N = 2560, 1280, 8, 128, 128
+S = E * C
+FLOPS = 2 * K * S * N
+
+F32 = mybir.dt.float32
+BF16 = mybir.dt.bfloat16
+I32 = mybir.dt.int32
+U32 = mybir.dt.uint32
+U16 = mybir.dt.uint16
+U8 = mybir.dt.uint8
+FP8X4 = mybir.dt.float8_e4m3fn_x4
+FP4X4 = mybir.dt.float4_e2m1fn_x4
+ACT = mybir.ActivationFunctionType
+MULT = mybir.AluOpType.mult
+
+P = 128
+PACK = 4
+K_PASS = P * PACK
+
+PASSES = (("e4m3", 0, 0, 4), ("e2m1", 0, 0, 0), ("e2m1", 1, 1, 0), ("e4m3", 1, 2, 4), ("e2m1", 2, 2, 0))
+QUANT = ((0, 512), (512, 768), (768, 1280))
+TAIL_QUANT = ((0, 512), (512, 1024), (1024, 1280))
+
+
+def tile_moe_two_lin_silu_kernel(
+    tc, xT, w8_words, w8_scales, w4_words, w4_scales, b, gate, offs, dst, out
+):
+    nc = tc.nc
+    last = len(PASSES) - 1
+    with ExitStack() as ctx:
+        keep = ctx.enter_context(tc.tile_pool(name="keep", bufs=1))
+        stage = ctx.enter_context(tc.tile_pool(name="stage", bufs=3))
+        psum = ctx.enter_context(tc.psum_pool(name="psum", bufs=1))
+
+        offs_sb = keep.tile([P, S // 16], U16, name="offs_sb")
+        dst_sb = keep.tile([P, S // 16], U16, name="dst_sb")
+        b_sb = keep.tile([P, E], F32, name="b_sb")
+        gate_sb = keep.tile([P, S], F32, name="gate_sb")
+        y_sb = keep.tile([P, S], F32, name="y_sb")
+        out_sb = keep.tile([P, T], F32, name="out_sb")
+        warm = keep.tile([P, 1], F32, name="warm")
+        raw = [keep.tile([P, PACK, T], F32, name=f"raw{i}") for i in range(len(PASSES))]
+        codes = [keep.tile([P, T], U32, name=f"codes{i}", align_bytes=64) for i in range(len(PASSES))]
+        planes = [keep.tile([P, T], U8, name=f"planes{i}", align_bytes=64) for i in range(3)]
+        slot_codes = [keep.tile([P, S], U32, name=f"slot_codes{i}", align_bytes=64) for i in range(len(PASSES))]
+        slot_planes = [keep.tile([P, S], U8, name=f"slot_planes{i}", align_bytes=64) for i in range(3)]
+        w8_sb = [keep.tile([P, E, 4 * N], U8, name=f"w8_sb{a}", align_bytes=64) for a in range(2)]
+        w4_sb = [keep.tile([P, E, 2 * N], U8, name=f"w4_sb{a}", align_bytes=64) for a in range(3)]
+        w8_plane = keep.tile([P, E * 2, N // 4], I32, name="w8_plane", align_bytes=64)
+        w4_plane = keep.tile([P, E * 3, N // 4], I32, name="w4_plane", align_bytes=64)
+        acc = [psum.tile([P, C], F32, name=f"acc{e}") for e in range(E)]
+
+        for plane in planes:
+            nc.gpsimd.memset(plane[:], 0)
+        nc.vector.memset(w8_plane[:], 0)
+        nc.vector.memset(w4_plane[:], 0)
+        nc.vector.memset(out_sb[:], 0.0)
+        nc.vector.memset(warm[:], 0.0)
+        nc.scalar.activation(warm[:], warm[:], ACT.Silu)
+
+        def load_x(i, c0, c1):
+            fmt, a, sp, k0 = PASSES[i]
+            row = K_PASS * a + (0 if fmt == "e4m3" else 1024)
+            src = xT[row : row + K_PASS, :].rearrange("(p j) w -> p j w", j=PACK)
+            nc.sync.dma_start(out=raw[i][:, :, c0:c1], in_=src[:, :, c0:c1])
+
+        def load_w8(a):
+            nc.sync.dma_start(
+                out=w8_sb[a][:].bitcast(I32),
+                in_=w8_words[:, a].rearrange("e p n r -> p e (n r)").bitcast(I32),
+            )
+
+        def load_w4(a):
+            nc.sync.dma_start(
+                out=w4_sb[a][:].bitcast(I32),
+                in_=w4_words[:, a].rearrange("e p n -> p e n").bitcast(I32),
+            )
+
+        def load_scales():
+            for tile, src in ((w8_plane, w8_scales), (w4_plane, w4_scales)):
+                rows = src.rearrange("e a q n -> q (e a) n").bitcast(I32)
+                for quad in range(4):
+                    nc.sync.dma_start(out=tile[32 * quad : 32 * quad + 4], in_=rows[4 * quad : 4 * quad + 4])
+
+        load_x(0, 0, 640)
+        nc.sync.dma_start(offs_sb[:], offs)
+        nc.sync.dma_start(dst_sb[:], dst)
+        nc.sync.dma_start(out=b_sb[:], in_=b)
+        load_x(0, 640, 1280)
+        load_x(1, 0, 768)
+        load_x(1, 768, T)
+        load_w8(0)
+        load_x(2, 0, 768)
+        load_x(2, 768, T)
+        load_w4(0)
+        load_w8(1)
+        load_x(3, 0, 768)
+        load_x(3, 768, T)
+        for c0, c1 in TAIL_QUANT:
+            load_x(last, c0, c1)
+        load_scales()
+        load_w4(1)
+        load_w4(2)
+        nc.sync.dma_start(out=gate_sb[:], in_=gate)
+
+        def interleave(engine, i, grouped, c0, c1):
+            src = raw[i][:, :, c0:c1].rearrange("p j w -> p w j")
+            if engine == "S":
+                nc.scalar.activation(grouped[:, c0:c1, :], src, ACT.Copy)
+            else:
+                nc.vector.tensor_copy(grouped[:, c0:c1, :], src)
+
+        def quantize(i, grouped, c0, c1):
+            fmt, a, sp, k0 = PASSES[i]
+            nc.vector.quantize_mx(
+                out=codes[i][:, c0:c1].bitcast(FP8X4),
+                scales=planes[sp][k0:P, c0:c1],
+                in_=grouped[:, c0:c1, :].rearrange("p w j -> p (w j)"),
+            )
+
+        def gather_codes(i, s0, s1):
+            nc.vector.tensor_copy(slot_codes[i][:, s0:s1], codes[i][:].indirect(offs_sb[:, s0 // 16 : s1 // 16]))
+
+        def gather_planes(sp, s0, s1):
+            nc.vector.tensor_copy(slot_planes[sp][:, s0:s1], planes[sp][:].indirect(offs_sb[:, s0 // 16 : s1 // 16]))
+
+        def multiply(i, e):
+            fmt, a, sp, k0 = PASSES[i]
+            cols = slice(e * C, (e + 1) * C)
+            if fmt == "e4m3":
+                w, plane = w8_sb[a][:, e, :].bitcast(FP8X4), w8_plane[:, 2 * e + a, :]
+            else:
+                w, plane = w4_sb[a][:, e, :].bitcast(FP4X4), w4_plane[:, 3 * e + a, :]
+            nc.tensor.matmul_mx(
+                out=acc[e][:],
+                lhsT=w,
+                lhsT_scale=plane.bitcast(U8),
+                rhs=slot_codes[i][:, cols].bitcast(FP8X4),
+                rhs_scale=slot_planes[sp][k0:P, cols],
+                start=(i == 0),
+                stop=(i == last),
+            )
+
+        SHARES = {0: (("S", 0, 384), ("V", 384, 640), ("S", 640, 1024), ("V", 1024, 1280))}
+        MIDDLE = (("S", 0, 512), ("S", 512, 768), ("S", 768, 1120), ("V", 1120, 1280))
+        TAIL = (("S", 0, 512), ("S", 512, 880), ("V", 880, 1024), ("S", 1024, 1120), ("V", 1120, 1280))
+        for i in range(len(PASSES)):
+            grouped = stage.tile([P, T, PACK], BF16, name="grouped", align_bytes=64)
+            for engine, c0, c1 in SHARES.get(i, TAIL if i == last else MIDDLE):
+                interleave(engine, i, grouped, c0, c1)
+            for c0, c1 in TAIL_QUANT if i == last else QUANT:
+                quantize(i, grouped, c0, c1)
+            if i < last:
+                gather_codes(i, 0, 512)
+                gather_codes(i, 512, 1024)
+            if i in (1, 2):
+                for s0 in (0, 512):
+                    gather_planes(i - 1, s0, s0 + 512)
+                for e in range(E):
+                    if i == 1:
+                        multiply(0, e)
+                    multiply(i, e)
+
+        for s in range(4):
+            gather_codes(last, s * 256, s * 256 + 256)
+            gather_planes(2, s * 256, s * 256 + 256)
+            for e in (2 * s, 2 * s + 1):
+                multiply(last - 1, e)
+                multiply(last, e)
+                nc.scalar.activation(y_sb[:, e * C : (e + 1) * C], acc[e][:], ACT.Silu, bias=b_sb[:, e : e + 1])
+        for s in range(4):
+            cols = slice(s * 256, s * 256 + 256)
+            nc.vector.tensor_tensor(out_sb[:].indirect(dst_sb[:, s * 16 : s * 16 + 16]), y_sb[:, cols], gate_sb[:, cols], MULT)
+        nc.sync.dma_start(out=out, in_=out_sb[:])

@@ -21,9 +21,16 @@ P = 128
 PACK = 4
 K_PASS = P * PACK
 
-PASSES = (("e4m3", 0, 0, 4), ("e2m1", 0, 0, 0), ("e2m1", 1, 1, 0), ("e4m3", 1, 2, 4), ("e2m1", 2, 2, 0))
-QUANT = ((0, 512), (512, 768), (768, 1280))
-TAIL_QUANT = ((0, 512), (512, 1024), (1024, 1280))
+PASSES = (("e2m1", 0, 0, 0), ("e2m1", 1, 0, 4), ("e4m3", 0, 1, 4), ("e4m3", 1, 1, 8), ("e2m1", 2, 1, 0))
+QUANT = {0: ((0, 512), (512, 1024), (1024, 1280)), 1: ((0, 512), (512, 1024), (1024, 1280)), 2: ((0, 512), (512, 1024), (1024, 1280)), 3: ((0, 512), (512, 1024), (1024, 1280)), 4: ((0, 512), (512, 1024), (1024, 1280))}
+LOADS = {0: ((0, 1280),), 1: ((0, 1280),), 2: ((0, 1280),), 3: ((0, 1280),), 4: ((0, 1280),)}
+COPIES = {
+    0: (("S", 0, 512), ("V", 512, 1280)),
+    1: (("V", 512, 1024), ("S", 0, 512), ("S", 1024, 1280)),
+    2: (("V", 1024, 1280), ("S", 0, 512), ("S", 512, 1024)),
+    3: (("V", 1024, 1280), ("S", 0, 512), ("S", 512, 1024)),
+    4: (("V", 0, 384), ("S", 384, 512), ("S", 512, 1024), ("S", 1024, 1280)),
+}
 
 
 def tile_moe_two_lin_silu_kernel(
@@ -45,19 +52,22 @@ def tile_moe_two_lin_silu_kernel(
         warm = keep.tile([P, 1], F32, name="warm")
         raw = [keep.tile([P, PACK, T], F32, name=f"raw{i}") for i in range(len(PASSES))]
         codes = [keep.tile([P, T], U32, name=f"codes{i}", align_bytes=64) for i in range(len(PASSES))]
-        planes = [keep.tile([P, T], U8, name=f"planes{i}", align_bytes=64) for i in range(3)]
+        planes = [keep.tile([P, T], U8, name=f"planes{i}", align_bytes=64) for i in range(2)]
         slot_codes = [keep.tile([P, S], U32, name=f"slot_codes{i}", align_bytes=64) for i in range(len(PASSES))]
-        slot_planes = [keep.tile([P, S], U8, name=f"slot_planes{i}", align_bytes=64) for i in range(3)]
-        w8_sb = [keep.tile([P, E, 4 * N], U8, name=f"w8_sb{a}", align_bytes=64) for a in range(2)]
-        w4_sb = [keep.tile([P, E, 2 * N], U8, name=f"w4_sb{a}", align_bytes=64) for a in range(3)]
+        slot_planes = [keep.tile([P, S], U8, name=f"slot_planes{i}", align_bytes=64) for i in range(2)]
+        moved_plane = keep.tile([P, S // 4], I32, name="moved_plane", align_bytes=64)
+        z_sb = keep.tile([P, S], F32, name="z_sb")
+        w8_sb = keep.tile([P, E * 2, 4 * N], U8, name="w8_sb", align_bytes=64)
+        w4_sb = keep.tile([P, E * 3, 2 * N], U8, name="w4_sb", align_bytes=64)
         w8_plane = keep.tile([P, E * 2, N // 4], I32, name="w8_plane", align_bytes=64)
         w4_plane = keep.tile([P, E * 3, N // 4], I32, name="w4_plane", align_bytes=64)
         acc = [psum.tile([P, C], F32, name=f"acc{e}") for e in range(E)]
 
-        for plane in planes:
-            nc.gpsimd.memset(plane[:], 0)
         nc.vector.memset(w8_plane[:], 0)
         nc.vector.memset(w4_plane[:], 0)
+        for plane in planes:
+            nc.gpsimd.memset(plane[:].bitcast(I32), 0)
+        nc.vector.memset(moved_plane[:], 0)
         nc.vector.memset(out_sb[:], 0.0)
         nc.vector.memset(warm[:], 0.0)
         nc.scalar.activation(warm[:], warm[:], ACT.Silu)
@@ -68,51 +78,57 @@ def tile_moe_two_lin_silu_kernel(
             src = xT[row : row + K_PASS, :].rearrange("(p j) w -> p j w", j=PACK)
             nc.sync.dma_start(out=raw[i][:, :, c0:c1], in_=src[:, :, c0:c1])
 
-        def load_w8(a):
-            nc.sync.dma_start(
-                out=w8_sb[a][:].bitcast(I32),
-                in_=w8_words[:, a].rearrange("e p n r -> p e (n r)").bitcast(I32),
+        def load_w8(e0, e1, queue=None):
+            (queue or nc.sync).dma_start(
+                out=w8_sb[:, 2 * e0 : 2 * e1, :].bitcast(I32),
+                in_=w8_words[e0:e1].rearrange("e a p n r -> p (e a) (n r)").bitcast(I32),
             )
 
-        def load_w4(a):
-            nc.sync.dma_start(
-                out=w4_sb[a][:].bitcast(I32),
-                in_=w4_words[:, a].rearrange("e p n -> p e n").bitcast(I32),
+        def load_w4(e0, e1, queue=None):
+            (queue or nc.sync).dma_start(
+                out=w4_sb[:, 3 * e0 : 3 * e1, :].bitcast(I32),
+                in_=w4_words[e0:e1].rearrange("e a p n -> p (e a) n").bitcast(I32),
             )
 
-        def load_scales():
+        def load_scales(queue):
             for tile, src in ((w8_plane, w8_scales), (w4_plane, w4_scales)):
                 rows = src.rearrange("e a q n -> q (e a) n").bitcast(I32)
                 for quad in range(4):
-                    nc.sync.dma_start(out=tile[32 * quad : 32 * quad + 4], in_=rows[4 * quad : 4 * quad + 4])
+                    queue.dma_start(out=tile[32 * quad : 32 * quad + 4], in_=rows[4 * quad : 4 * quad + 4])
 
-        load_x(0, 0, 640)
-        nc.sync.dma_start(offs_sb[:], offs)
-        nc.sync.dma_start(dst_sb[:], dst)
-        nc.sync.dma_start(out=b_sb[:], in_=b)
-        load_x(0, 640, 1280)
-        load_x(1, 0, 768)
-        load_x(1, 768, T)
-        load_w8(0)
-        load_x(2, 0, 768)
-        load_x(2, 768, T)
-        load_w4(0)
-        load_w8(1)
-        load_x(3, 0, 768)
-        load_x(3, 768, T)
-        for c0, c1 in TAIL_QUANT:
-            load_x(last, c0, c1)
-        load_scales()
-        load_w4(1)
-        load_w4(2)
-        nc.sync.dma_start(out=gate_sb[:], in_=gate)
+        def load_lists():
+            nc.sync.dma_start(offs_sb[:], offs)
+            nc.sync.dma_start(dst_sb[:], dst)
+
+        def load_gate(queue=None):
+            (queue or nc.sync).dma_start(out=gate_sb[:], in_=gate)
+
+        def load_b(queue):
+            queue.dma_start(out=b_sb[:], in_=b)
+
+        def load_pass(i):
+            for c0, c1 in LOADS[i]:
+                load_x(i, c0, c1)
+
+        load_scales(nc.gpsimd)
+        load_b(nc.gpsimd)
+        load_pass(0)
+        load_lists()
+        for i in range(1, len(PASSES)):
+            load_pass(i)
+        load_w4(0, E)
+        load_w8(0, E)
+        load_gate()
 
         def interleave(engine, i, grouped, c0, c1):
-            src = raw[i][:, :, c0:c1].rearrange("p j w -> p w j")
+            dst_view = grouped[:, c0:c1, :].rearrange("p (c i) t -> p c t i", i=4)
+            src_view = raw[i][:, :, c0:c1].rearrange("p t (c i) -> p c t i", i=4)
+            if False:
+                dst_view, src_view = grouped[:, c0:c1, :], raw[i][:, :, c0:c1].rearrange("p j w -> p w j")
             if engine == "S":
-                nc.scalar.activation(grouped[:, c0:c1, :], src, ACT.Copy)
+                nc.scalar.activation(dst_view, src_view, ACT.Copy)
             else:
-                nc.vector.tensor_copy(grouped[:, c0:c1, :], src)
+                nc.vector.tensor_copy(dst_view, src_view)
 
         def quantize(i, grouped, c0, c1):
             fmt, a, sp, k0 = PASSES[i]
@@ -132,47 +148,55 @@ def tile_moe_two_lin_silu_kernel(
             fmt, a, sp, k0 = PASSES[i]
             cols = slice(e * C, (e + 1) * C)
             if fmt == "e4m3":
-                w, plane = w8_sb[a][:, e, :].bitcast(FP8X4), w8_plane[:, 2 * e + a, :]
+                w, plane = w8_sb[:, 2 * e + a, :].bitcast(FP8X4), w8_plane[:, 2 * e + a, :]
             else:
-                w, plane = w4_sb[a][:, e, :].bitcast(FP4X4), w4_plane[:, 3 * e + a, :]
+                w, plane = w4_sb[:, 3 * e + a, :].bitcast(FP4X4), w4_plane[:, 3 * e + a, :]
+            if fmt == "e2m1" and k0 == 4:
+                rhs_scale = moved_plane[:].bitcast(U8)[:, cols]
+            else:
+                rhs_scale = slot_planes[sp][k0:P, cols]
             nc.tensor.matmul_mx(
                 out=acc[e][:],
                 lhsT=w,
                 lhsT_scale=plane.bitcast(U8),
                 rhs=slot_codes[i][:, cols].bitcast(FP8X4),
-                rhs_scale=slot_planes[sp][k0:P, cols],
+                rhs_scale=rhs_scale,
                 start=(i == 0),
                 stop=(i == last),
             )
 
-        SHARES = {0: (("S", 0, 384), ("V", 384, 640), ("S", 640, 1024), ("V", 1024, 1280))}
-        MIDDLE = (("S", 0, 512), ("S", 512, 768), ("S", 768, 1120), ("V", 1120, 1280))
-        TAIL = (("S", 0, 512), ("S", 512, 880), ("V", 880, 1024), ("S", 1024, 1120), ("V", 1120, 1280))
         for i in range(len(PASSES)):
             grouped = stage.tile([P, T, PACK], BF16, name="grouped", align_bytes=64)
-            for engine, c0, c1 in SHARES.get(i, TAIL if i == last else MIDDLE):
+            for engine, c0, c1 in COPIES[i]:
                 interleave(engine, i, grouped, c0, c1)
-            for c0, c1 in TAIL_QUANT if i == last else QUANT:
+            if i == last:
+                for quad in range(4):
+                    nc.scalar.dma_start(
+                        out=moved_plane[32 * quad : 32 * quad + 4],
+                        in_=slot_planes[0][32 * quad + 4 : 32 * quad + 8].bitcast(I32),
+                    )
+                for e in range(E):
+                    multiply(0, e)
+                    multiply(1, e)
+            for c0, c1 in QUANT[i]:
                 quantize(i, grouped, c0, c1)
             if i < last:
                 gather_codes(i, 0, 512)
                 gather_codes(i, 512, 1024)
-            if i in (1, 2):
+            if i == 1:
                 for s0 in (0, 512):
-                    gather_planes(i - 1, s0, s0 + 512)
-                for e in range(E):
-                    if i == 1:
-                        multiply(0, e)
-                    multiply(i, e)
+                    gather_planes(0, s0, s0 + 512)
 
         for s in range(4):
             gather_codes(last, s * 256, s * 256 + 256)
-            gather_planes(2, s * 256, s * 256 + 256)
+            gather_planes(1, s * 256, s * 256 + 256)
+        for s in range(4):
             for e in (2 * s, 2 * s + 1):
-                multiply(last - 1, e)
-                multiply(last, e)
+                for i in range(2, last + 1):
+                    multiply(i, e)
                 nc.scalar.activation(y_sb[:, e * C : (e + 1) * C], acc[e][:], ACT.Silu, bias=b_sb[:, e : e + 1])
         for s in range(4):
             cols = slice(s * 256, s * 256 + 256)
-            nc.vector.tensor_tensor(out_sb[:].indirect(dst_sb[:, s * 16 : s * 16 + 16]), y_sb[:, cols], gate_sb[:, cols], MULT)
+            nc.vector.tensor_tensor(z_sb[:, cols], y_sb[:, cols], gate_sb[:, cols], MULT)
+            nc.vector.tensor_copy(out_sb[:].indirect(dst_sb[:, s * 16 : s * 16 + 16]), z_sb[:, cols])
         nc.sync.dma_start(out=out, in_=out_sb[:])

@@ -21,15 +21,15 @@ P = 128
 PACK = 4
 K_PASS = P * PACK
 
-PASSES = (("e2m1", 0, 0, 0), ("e2m1", 1, 0, 4), ("e4m3", 0, 1, 4), ("e4m3", 1, 1, 8), ("e2m1", 2, 1, 0))
+PASSES = (("e2m1", 0, 0, 0), ("e2m1", 1, 1, 0), ("e4m3", 0, 2, 4), ("e4m3", 1, 2, 8), ("e2m1", 2, 2, 0))
 QUANT = {0: ((0, 512), (512, 1024), (1024, 1280)), 1: ((0, 512), (512, 1024), (1024, 1280)), 2: ((0, 512), (512, 1024), (1024, 1280)), 3: ((0, 512), (512, 1024), (1024, 1280)), 4: ((0, 512), (512, 1024), (1024, 1280))}
-LOADS = {0: ((0, 1280),), 1: ((0, 1280),), 2: ((0, 1280),), 3: ((0, 1280),), 4: ((0, 1280),)}
+LOADS = {0: ((0, 512), (512, 1280)), 1: ((0, 512), (512, 1280)), 2: ((0, 1280),), 3: ((0, 1280),), 4: ((0, 1280),)}
 COPIES = {
-    0: (("S", 0, 512), ("V", 512, 1280)),
-    1: (("V", 512, 1024), ("S", 0, 512), ("S", 1024, 1280)),
-    2: (("V", 1024, 1280), ("S", 0, 512), ("S", 512, 1024)),
-    3: (("V", 1024, 1280), ("S", 0, 512), ("S", 512, 1024)),
-    4: (("V", 0, 384), ("S", 384, 512), ("S", 512, 1024), ("S", 1024, 1280)),
+    0: (("S", 0, 512), ("V", 768, 1280), ("S", 512, 768)),
+    1: (("S", 0, 512), ("V", 1024, 1280), ("S", 512, 1024)),
+    2: (("V", 896, 1280), ("S", 0, 512), ("S", 512, 896)),
+    3: (("V", 896, 1280), ("S", 0, 512), ("S", 512, 896)),
+    4: (("V", 896, 1280), ("S", 0, 512), ("S", 512, 896)),
 }
 
 
@@ -40,7 +40,7 @@ def tile_moe_two_lin_silu_kernel(
     last = len(PASSES) - 1
     with ExitStack() as ctx:
         keep = ctx.enter_context(tc.tile_pool(name="keep", bufs=1))
-        stage = ctx.enter_context(tc.tile_pool(name="stage", bufs=3))
+        stage = ctx.enter_context(tc.tile_pool(name="stage", bufs=5))
         psum = ctx.enter_context(tc.psum_pool(name="psum", bufs=1))
 
         offs_sb = keep.tile([P, S // 16], U16, name="offs_sb")
@@ -52,11 +52,9 @@ def tile_moe_two_lin_silu_kernel(
         warm = keep.tile([P, 1], F32, name="warm")
         raw = [keep.tile([P, PACK, T], F32, name=f"raw{i}") for i in range(len(PASSES))]
         codes = [keep.tile([P, T], U32, name=f"codes{i}", align_bytes=64) for i in range(len(PASSES))]
-        planes = [keep.tile([P, T], U8, name=f"planes{i}", align_bytes=64) for i in range(2)]
+        planes = [keep.tile([P, T], U8, name=f"planes{i}", align_bytes=64) for i in range(3)]
         slot_codes = [keep.tile([P, S], U32, name=f"slot_codes{i}", align_bytes=64) for i in range(len(PASSES))]
-        slot_planes = [keep.tile([P, S], U8, name=f"slot_planes{i}", align_bytes=64) for i in range(2)]
-        moved_plane = keep.tile([P, S // 4], I32, name="moved_plane", align_bytes=64)
-        z_sb = keep.tile([P, S], F32, name="z_sb")
+        slot_planes = [keep.tile([P, S], U8, name=f"slot_planes{i}", align_bytes=64) for i in range(3)]
         w8_sb = keep.tile([P, E * 2, 4 * N], U8, name="w8_sb", align_bytes=64)
         w4_sb = keep.tile([P, E * 3, 2 * N], U8, name="w4_sb", align_bytes=64)
         w8_plane = keep.tile([P, E * 2, N // 4], I32, name="w8_plane", align_bytes=64)
@@ -64,10 +62,9 @@ def tile_moe_two_lin_silu_kernel(
         acc = [psum.tile([P, C], F32, name=f"acc{e}") for e in range(E)]
 
         nc.vector.memset(w8_plane[:], 0)
-        nc.vector.memset(w4_plane[:], 0)
+        nc.gpsimd.memset(w4_plane[:], 0)
         for plane in planes:
             nc.gpsimd.memset(plane[:].bitcast(I32), 0)
-        nc.vector.memset(moved_plane[:], 0)
         nc.vector.memset(out_sb[:], 0.0)
         nc.vector.memset(warm[:], 0.0)
         nc.scalar.activation(warm[:], warm[:], ACT.Silu)
@@ -90,11 +87,10 @@ def tile_moe_two_lin_silu_kernel(
                 in_=w4_words[e0:e1].rearrange("e a p n -> p (e a) n").bitcast(I32),
             )
 
-        def load_scales(queue):
-            for tile, src in ((w8_plane, w8_scales), (w4_plane, w4_scales)):
-                rows = src.rearrange("e a q n -> q (e a) n").bitcast(I32)
-                for quad in range(4):
-                    queue.dma_start(out=tile[32 * quad : 32 * quad + 4], in_=rows[4 * quad : 4 * quad + 4])
+        def load_scale_rows(tile, src):
+            rows = src.rearrange("e a q n -> q (e a) n").bitcast(I32)
+            for quad in range(4):
+                nc.sync.dma_start(out=tile[32 * quad : 32 * quad + 4], in_=rows[4 * quad : 4 * quad + 4])
 
         def load_lists():
             nc.sync.dma_start(offs_sb[:], offs)
@@ -110,20 +106,21 @@ def tile_moe_two_lin_silu_kernel(
             for c0, c1 in LOADS[i]:
                 load_x(i, c0, c1)
 
-        load_scales(nc.gpsimd)
-        load_b(nc.gpsimd)
         load_pass(0)
         load_lists()
+        load_b(nc.sync)
         for i in range(1, len(PASSES)):
             load_pass(i)
+        load_scale_rows(w4_plane, w4_scales)
         load_w4(0, E)
+        load_scale_rows(w8_plane, w8_scales)
         load_w8(0, E)
         load_gate()
 
         def interleave(engine, i, grouped, c0, c1):
             dst_view = grouped[:, c0:c1, :].rearrange("p (c i) t -> p c t i", i=4)
             src_view = raw[i][:, :, c0:c1].rearrange("p t (c i) -> p c t i", i=4)
-            if False:
+            if True:
                 dst_view, src_view = grouped[:, c0:c1, :], raw[i][:, :, c0:c1].rearrange("p j w -> p w j")
             if engine == "S":
                 nc.scalar.activation(dst_view, src_view, ACT.Copy)
@@ -151,16 +148,12 @@ def tile_moe_two_lin_silu_kernel(
                 w, plane = w8_sb[:, 2 * e + a, :].bitcast(FP8X4), w8_plane[:, 2 * e + a, :]
             else:
                 w, plane = w4_sb[:, 3 * e + a, :].bitcast(FP4X4), w4_plane[:, 3 * e + a, :]
-            if fmt == "e2m1" and k0 == 4:
-                rhs_scale = moved_plane[:].bitcast(U8)[:, cols]
-            else:
-                rhs_scale = slot_planes[sp][k0:P, cols]
             nc.tensor.matmul_mx(
                 out=acc[e][:],
                 lhsT=w,
                 lhsT_scale=plane.bitcast(U8),
                 rhs=slot_codes[i][:, cols].bitcast(FP8X4),
-                rhs_scale=rhs_scale,
+                rhs_scale=slot_planes[sp][k0:P, cols],
                 start=(i == 0),
                 stop=(i == last),
             )
@@ -169,34 +162,28 @@ def tile_moe_two_lin_silu_kernel(
             grouped = stage.tile([P, T, PACK], BF16, name="grouped", align_bytes=64)
             for engine, c0, c1 in COPIES[i]:
                 interleave(engine, i, grouped, c0, c1)
-            if i == last:
-                for quad in range(4):
-                    nc.scalar.dma_start(
-                        out=moved_plane[32 * quad : 32 * quad + 4],
-                        in_=slot_planes[0][32 * quad + 4 : 32 * quad + 8].bitcast(I32),
-                    )
-                for e in range(E):
-                    multiply(0, e)
-                    multiply(1, e)
             for c0, c1 in QUANT[i]:
                 quantize(i, grouped, c0, c1)
             if i < last:
                 gather_codes(i, 0, 512)
                 gather_codes(i, 512, 1024)
-            if i == 1:
+            if i in (0, 1):
                 for s0 in (0, 512):
-                    gather_planes(0, s0, s0 + 512)
+                    gather_planes(i, s0, s0 + 512)
+            if i == 1:
+                for e in range(E):
+                    multiply(0, e)
+                    multiply(1, e)
 
-        for s in range(4):
-            gather_codes(last, s * 256, s * 256 + 256)
-            gather_planes(1, s * 256, s * 256 + 256)
+        for s in range(2):
+            gather_codes(last, s * 512, s * 512 + 512)
+            gather_planes(2, s * 512, s * 512 + 512)
         for s in range(4):
             for e in (2 * s, 2 * s + 1):
                 for i in range(2, last + 1):
                     multiply(i, e)
                 nc.scalar.activation(y_sb[:, e * C : (e + 1) * C], acc[e][:], ACT.Silu, bias=b_sb[:, e : e + 1])
-        for s in range(4):
-            cols = slice(s * 256, s * 256 + 256)
-            nc.vector.tensor_tensor(z_sb[:, cols], y_sb[:, cols], gate_sb[:, cols], MULT)
-            nc.vector.tensor_copy(out_sb[:].indirect(dst_sb[:, s * 16 : s * 16 + 16]), z_sb[:, cols])
+        for s in range(2):
+            cols = slice(s * 512, s * 512 + 512)
+            nc.vector.tensor_tensor(out_sb[:].indirect(dst_sb[:, s * 32 : s * 32 + 32]), y_sb[:, cols], gate_sb[:, cols], MULT)
         nc.sync.dma_start(out=out, in_=out_sb[:])

from contextlib import ExitStack

import concourse.mybir as mybir

K, T, E, C, N = 2560, 1280, 8, 128, 128
S = E * C
FLOPS = 2 * K * S * N

F32 = mybir.dt.float32
BF16 = mybir.dt.bfloat16
I32 = mybir.dt.int32
U32 = mybir.dt.uint32
U16 = mybir.dt.uint16
U8 = mybir.dt.uint8
FP8X4 = mybir.dt.float8_e4m3fn_x4
FP4X4 = mybir.dt.float4_e2m1fn_x4
ACT = mybir.ActivationFunctionType
MULT = mybir.AluOpType.mult

P = 128
PACK = 4
K_PASS = P * PACK

PASSES = (("e2m1", 0, 0, 0), ("e2m1", 1, 1, 0), ("e4m3", 0, 2, 4), ("e4m3", 1, 2, 8), ("e2m1", 2, 2, 0))
QUANT = {0: ((0, 512), (512, 1024), (1024, 1280)), 1: ((0, 512), (512, 1024), (1024, 1280)), 2: ((0, 512), (512, 1024), (1024, 1280)), 3: ((0, 512), (512, 1024), (1024, 1280)), 4: ((0, 512), (512, 1024), (1024, 1280))}
LOADS = {0: ((0, 512), (512, 1280)), 1: ((0, 512), (512, 1280)), 2: ((0, 1280),), 3: ((0, 1280),), 4: ((0, 1280),)}
COPIES = {
    0: (("S", 0, 512), ("V", 768, 1280), ("S", 512, 768)),
    1: (("S", 0, 512), ("V", 1024, 1280), ("S", 512, 1024)),
    2: (("V", 896, 1280), ("S", 0, 512), ("S", 512, 896)),
    3: (("V", 896, 1280), ("S", 0, 512), ("S", 512, 896)),
    4: (("V", 896, 1280), ("S", 0, 512), ("S", 512, 896)),
}


def tile_moe_two_lin_silu_kernel(
    tc, xT, w8_words, w8_scales, w4_words, w4_scales, b, gate, offs, dst, out
):
    nc = tc.nc
    last = len(PASSES) - 1
    with ExitStack() as ctx:
        keep = ctx.enter_context(tc.tile_pool(name="keep", bufs=1))
        stage = ctx.enter_context(tc.tile_pool(name="stage", bufs=5))
        psum = ctx.enter_context(tc.psum_pool(name="psum", bufs=1))

        offs_sb = keep.tile([P, S // 16], U16, name="offs_sb")
        dst_sb = keep.tile([P, S // 16], U16, name="dst_sb")
        b_sb = keep.tile([P, E], F32, name="b_sb")
        gate_sb = keep.tile([P, S], F32, name="gate_sb")
        y_sb = keep.tile([P, S], F32, name="y_sb")
        out_sb = keep.tile([P, T], F32, name="out_sb")
        warm = keep.tile([P, 1], F32, name="warm")
        raw = [keep.tile([P, PACK, T], F32, name=f"raw{i}") for i in range(len(PASSES))]
        codes = [keep.tile([P, T], U32, name=f"codes{i}", align_bytes=64) for i in range(len(PASSES))]
        planes = [keep.tile([P, T], U8, name=f"planes{i}", align_bytes=64) for i in range(3)]
        slot_codes = [keep.tile([P, S], U32, name=f"slot_codes{i}", align_bytes=64) for i in range(len(PASSES))]
        slot_planes = [keep.tile([P, S], U8, name=f"slot_planes{i}", align_bytes=64) for i in range(3)]
        w8_sb = keep.tile([P, E * 2, 4 * N], U8, name="w8_sb", align_bytes=64)
        w4_sb = keep.tile([P, E * 3, 2 * N], U8, name="w4_sb", align_bytes=64)
        w8_plane = keep.tile([P, E * 2, N // 4], I32, name="w8_plane", align_bytes=64)
        w4_plane = keep.tile([P, E * 3, N // 4], I32, name="w4_plane", align_bytes=64)
        acc = [psum.tile([P, C], F32, name=f"acc{e}") for e in range(E)]

        nc.vector.memset(w8_plane[:], 0)
        nc.gpsimd.memset(w4_plane[:], 0)
        for plane in planes:
            nc.gpsimd.memset(plane[:].bitcast(I32), 0)
        nc.vector.memset(out_sb[:], 0.0)
        nc.vector.memset(warm[:], 0.0)
        nc.scalar.activation(warm[:], warm[:], ACT.Silu)

        def load_x(i, c0, c1):
            fmt, a, sp, k0 = PASSES[i]
            row = K_PASS * a + (0 if fmt == "e4m3" else 1024)
            src = xT[row : row + K_PASS, :].rearrange("(p j) w -> p j w", j=PACK)
            nc.sync.dma_start(out=raw[i][:, :, c0:c1], in_=src[:, :, c0:c1])

        def load_w8(e0, e1, queue=None):
            (queue or nc.sync).dma_start(
                out=w8_sb[:, 2 * e0 : 2 * e1, :].bitcast(I32),
                in_=w8_words[e0:e1].rearrange("e a p n r -> p (e a) (n r)").bitcast(I32),
            )

        def load_w4(e0, e1, queue=None):
            (queue or nc.sync).dma_start(
                out=w4_sb[:, 3 * e0 : 3 * e1, :].bitcast(I32),
                in_=w4_words[e0:e1].rearrange("e a p n -> p (e a) n").bitcast(I32),
            )

        def load_scale_rows(tile, src):
            rows = src.rearrange("e a q n -> q (e a) n").bitcast(I32)
            for quad in range(4):
                nc.sync.dma_start(out=tile[32 * quad : 32 * quad + 4], in_=rows[4 * quad : 4 * quad + 4])

        def load_lists():
            nc.sync.dma_start(offs_sb[:], offs)
            nc.sync.dma_start(dst_sb[:], dst)

        def load_gate(queue=None):
            (queue or nc.sync).dma_start(out=gate_sb[:], in_=gate)

        def load_b(queue):
            queue.dma_start(out=b_sb[:], in_=b)

        def load_pass(i):
            for c0, c1 in LOADS[i]:
                load_x(i, c0, c1)

        load_pass(0)
        load_lists()
        load_b(nc.sync)
        for i in range(1, len(PASSES)):
            load_pass(i)
        load_scale_rows(w4_plane, w4_scales)
        load_w4(0, E)
        load_scale_rows(w8_plane, w8_scales)
        load_w8(0, E)
        load_gate()

        def interleave(engine, i, grouped, c0, c1):
            dst_view = grouped[:, c0:c1, :].rearrange("p (c i) t -> p c t i", i=4)
            src_view = raw[i][:, :, c0:c1].rearrange("p t (c i) -> p c t i", i=4)
            if True:
                dst_view, src_view = grouped[:, c0:c1, :], raw[i][:, :, c0:c1].rearrange("p j w -> p w j")
            if engine == "S":
                nc.scalar.activation(dst_view, src_view, ACT.Copy)
            else:
                nc.vector.tensor_copy(dst_view, src_view)

        def quantize(i, grouped, c0, c1):
            fmt, a, sp, k0 = PASSES[i]
            nc.vector.quantize_mx(
                out=codes[i][:, c0:c1].bitcast(FP8X4),
                scales=planes[sp][k0:P, c0:c1],
                in_=grouped[:, c0:c1, :].rearrange("p w j -> p (w j)"),
            )

        def gather_codes(i, s0, s1):
            nc.vector.tensor_copy(slot_codes[i][:, s0:s1], codes[i][:].indirect(offs_sb[:, s0 // 16 : s1 // 16]))

        def gather_planes(sp, s0, s1):
            nc.vector.tensor_copy(slot_planes[sp][:, s0:s1], planes[sp][:].indirect(offs_sb[:, s0 // 16 : s1 // 16]))

        def multiply(i, e):
            fmt, a, sp, k0 = PASSES[i]
            cols = slice(e * C, (e + 1) * C)
            if fmt == "e4m3":
                w, plane = w8_sb[:, 2 * e + a, :].bitcast(FP8X4), w8_plane[:, 2 * e + a, :]
            else:
                w, plane = w4_sb[:, 3 * e + a, :].bitcast(FP4X4), w4_plane[:, 3 * e + a, :]
            nc.tensor.matmul_mx(
                out=acc[e][:],
                lhsT=w,
                lhsT_scale=plane.bitcast(U8),
                rhs=slot_codes[i][:, cols].bitcast(FP8X4),
                rhs_scale=slot_planes[sp][k0:P, cols],
                start=(i == 0),
                stop=(i == last),
            )

        for i in range(len(PASSES)):
            grouped = stage.tile([P, T, PACK], BF16, name="grouped", align_bytes=64)
            for engine, c0, c1 in COPIES[i]:
                interleave(engine, i, grouped, c0, c1)
            for c0, c1 in QUANT[i]:
                quantize(i, grouped, c0, c1)
            if i < last:
                gather_codes(i, 0, 512)
                gather_codes(i, 512, 1024)
            if i in (0, 1):
                for s0 in (0, 512):
                    gather_planes(i, s0, s0 + 512)
            if i == 1:
                for e in range(E):
                    multiply(0, e)
                    multiply(1, e)

        for s in range(2):
            gather_codes(last, s * 512, s * 512 + 512)
            gather_planes(2, s * 512, s * 512 + 512)
        for s in range(4):
            for e in (2 * s, 2 * s + 1):
                for i in range(2, last + 1):
                    multiply(i, e)
                nc.scalar.activation(y_sb[:, e * C : (e + 1) * C], acc[e][:], ACT.Silu, bias=b_sb[:, e : e + 1])
        for s in range(2):
            cols = slice(s * 512, s * 512 + 512)
            nc.vector.tensor_tensor(out_sb[:].indirect(dst_sb[:, s * 32 : s * 32 + 32]), y_sb[:, cols], gate_sb[:, cols], MULT)
        nc.sync.dma_start(out=out, in_=out_sb[:])
